import numpy as np
import ml_dtypes


def mxq(x, axis, fmt="e4m3"):
    dtype, down = {"e4m3": (ml_dtypes.float8_e4m3fn, 7), "e5m2": (ml_dtypes.float8_e5m2, 14)}[fmt]
    v = np.moveaxis(np.asarray(x, np.float32).astype(ml_dtypes.bfloat16).astype(np.float64), axis, -1)
    blocks = v.reshape(v.shape[:-1] + (-1, 32))
    amax = np.abs(blocks).max(-1, keepdims=True)
    byte = np.maximum(np.where(amax > 0, np.frexp(amax)[1] - 1 + 127, 0) - down, 1)
    scale = np.exp2(byte - 127.0)
    codes = (blocks / scale).astype(np.float32).astype(dtype).astype(np.float64)
    return np.moveaxis((codes * scale).reshape(v.shape), -1, axis)


WIDE = False


def mx_kscale(k):
    if not WIDE:
        return np.ones(k)
    levels = np.array([10, -10, 5, -5, 0])
    if k % 512:
        return np.exp2(np.random.permutation(np.resize(levels, k // 32))).repeat(32)
    a = np.empty((k // 512, 16))
    for p in range(k // 512):
        a[p, :8] = np.random.permutation(np.resize(levels, 8))
        for g in range(8):
            far = levels[np.abs(levels - a[p, g]) >= 10]
            a[p, g + 8] = far[np.random.randint(len(far))]
    return np.exp2(a.ravel()).repeat(32)


def f64(x):
    return np.asarray(x).astype(np.float64)


def striped(idx):
    return np.tile(np.asarray(idx).reshape(-1, 16).T, (8, 1)).astype(np.uint16)


def unstriped(offs):
    return offs[:16].T.reshape(-1).astype(np.int64)


E2M1 = np.array([0.0, 0.5, 1.0, 1.5, 2.0, 3.0, 4.0, 6.0, -0.0, -0.5, -1.0, -1.5, -2.0, -3.0, -4.0, -6.0])


def pack_weight(w, fmt):
    k, n = w.shape
    w = f64(np.asarray(w, np.float32).astype(ml_dtypes.bfloat16)).reshape(k // 32, 32, n)
    amax = np.abs(w).max(1)
    if fmt == "e4m3":
        byte = np.frexp(amax)[1] - 1 + 127 - 7
    else:
        mant, ex = np.frexp(amax / 6.0)
        byte = np.where(mant > 0.5, ex, ex - 1) + 127
    byte = np.clip(np.where(amax > 0, byte, 1), 1, 254)
    scaled = (w * np.exp2(127.0 - byte)[:, None, :]).reshape(k, n).astype(np.float32)
    by_word = np.ascontiguousarray(scaled.reshape(k // 512, 128, 4, n).transpose(0, 1, 3, 2))
    if fmt == "e4m3":
        words = by_word.astype(ml_dtypes.float8_e4m3fn).view(np.uint8)
    else:
        c = by_word.astype(ml_dtypes.float4_e2m1fn).view(np.uint8) & 0xF
        words = (c[..., 0::2] | (c[..., 1::2] << 4)).reshape(k // 512, 128, 2 * n)
    return np.ascontiguousarray(words), np.ascontiguousarray(byte.astype(np.uint8).reshape(k // 512, 16, n))


def unpack_weight(words, scales, fmt):
    g, _, n = scales.shape
    words = np.ascontiguousarray(words).reshape(g, 128, n, -1)
    if fmt == "e4m3":
        vals = words.view(ml_dtypes.float8_e4m3fn).astype(np.float64)
    else:
        nib = np.empty((g, 128, n, 4), np.uint8)
        nib[..., 0::2] = words & 0xF
        nib[..., 1::2] = words >> 4
        vals = E2M1[nib]
    vals = vals * np.repeat(np.exp2(scales.astype(np.float64) - 127.0), 8, axis=1)[..., None]
    return vals.transpose(0, 1, 3, 2).reshape(g * 512, n)


D, T, I, Q, E = 512, 2048, 512, 128, 512


def setup_inputs():
    n = np.random.standard_normal
    idx = np.random.permutation(T)[:I]
    fd = mx_kscale(D)
    fi = mx_kscale(I)
    ti = np.ones(T)
    ti[idx] = fi
    keysp = pack_weight(n((D, T)) / fd[:, None], "e4m3")
    return {
        "query": (n((D, Q)) * 0.2 / np.sqrt(D) * fd[:, None]).astype(np.float32),
        "keys_words": keysp[0],
        "keys_scales": keysp[1],
        "age": np.tile(np.random.uniform(0.0, 2.0, T), (128, 1)).astype(np.float32),
        "rate": (np.random.uniform(0.3, 1.2, (Q, 1))).astype(np.float32),
        "reserve": (np.random.uniform(20.0, 100.0, (Q, 1))).astype(np.float32),
        "size": (np.random.uniform(0.5, 2.0, (1, I)) * fi).astype(np.float32),
        "vals": (n((E, T)) / ti).astype(np.float32),
        "offs": striped(idx),
    }


def reference(query, keys_words, keys_scales, age, rate, reserve, size, vals, offs):
    idx = unstriped(offs)
    keysu = unpack_weight(keys_words, keys_scales, "e4m3")
    queryq = mxq(f64(query), 0, "e4m3")
    keysidxg = keysu[:, idx]
    a = queryq.T @ keysidxg
    p = np.exp(a - np.max(a, axis=1, keepdims=True)) * np.exp(f64(age)[:1][:, idx] * f64(rate) * (-1.0))
    w = p * f64(size) / (np.sum(p, axis=1, keepdims=True) + f64(reserve))
    wt = w.T
    vt = f64(vals)[:, idx].T
    wtq = mxq(wt, 0, "e4m3")
    vtq = mxq(vt, 0, "e4m3")
    o = wtq.T @ vtq
    return o

@@ -1,0 +1,164 @@
+from contextlib import ExitStack
+
+import concourse.mybir as mybir
+from concourse.masks import make_identity
+
+D, T, I, Q, E = 512, 2048, 512, 128, 512
+FLOPS = 2 * Q * I * D + 2 * Q * I * E
+BYTES = 4 * (D * Q + T + 2 * Q + I + E * T + Q * E) + D * T + 16 * T + 2 * 128 * 32
+
+F32 = mybir.dt.float32
+BF16 = mybir.dt.bfloat16
+I32 = mybir.dt.int32
+U32 = mybir.dt.uint32
+U16 = mybir.dt.uint16
+U8 = mybir.dt.uint8
+FP8X4 = mybir.dt.float8_e4m3fn_x4
+ALU = mybir.AluOpType
+ACT = mybir.ActivationFunctionType
+AXIS = mybir.AxisListType
+
+P = 128
+PACK = 4
+BANK = 512
+
+
+def tile_attend_massfade_kernel(tc, query, keys_words, keys_scales, age, rate, reserve, size, vals, offs, out):
+    nc = tc.nc
+    with ExitStack() as ctx:
+        keep = ctx.enter_context(tc.tile_pool(name="keep", bufs=1))
+        turn = ctx.enter_context(tc.psum_pool(name="turn", bufs=3))
+        psum = ctx.enter_context(tc.psum_pool(name="psum", bufs=1))
+
+        offsets = keep.tile([P, I // 16], U16, name="offsets")
+        nc.sync.dma_start(offsets[:], offs)
+
+        kscale_pool = keep.tile([P, T], U8, name="kscale_pool")
+        nc.gpsimd.memset(kscale_pool[:].bitcast(I32), 0)
+
+        age_cols = keep.tile([P, T // P], F32, name="age_cols")
+        nc.sync.dma_start(age_cols[:], age[0, :].rearrange("(p j) -> p j", p=P))
+        q_raw = keep.tile([P, PACK, Q], F32, name="q_raw")
+        nc.sync.dma_start(q_raw[:], query.rearrange("(p j) q -> p j q", j=PACK))
+        for g in range(4):
+            nc.sync.dma_start(
+                kscale_pool[32 * g : 32 * g + 4, :].bitcast(I32), keys_scales[0, 4 * g : 4 * g + 4, :].bitcast(I32)
+            )
+        kword_pool = keep.tile([P, T], U32, name="kword_pool")
+        nc.sync.dma_start(kword_pool[:].bitcast(I32), keys_words[0].rearrange("p n t -> p (n t)").bitcast(I32))
+        size_cols = keep.tile([P, PACK], F32, name="size_cols")
+        nc.sync.dma_start(size_cols[:], size[0, :].rearrange("(p j) -> p j", p=P))
+        rate_col = keep.tile([P, 1], F32, name="rate_col")
+        nc.sync.dma_start(rate_col[:], rate)
+        reserve_col = keep.tile([P, 1], F32, name="reserve_col")
+        nc.sync.dma_start(reserve_col[:], reserve)
+        val_pool = [keep.tile([P, T], F32, name="val_pool%d" % b, align_bytes=64) for b in range(E // P)]
+        for b in range(E // P):
+            nc.sync.dma_start(val_pool[b][:], vals[b * P : (b + 1) * P, :])
+
+        ident = keep.tile([P, P], F32, name="ident")
+        make_identity(nc, ident[:])
+
+        warm = keep.tile([P, 1], F32, name="warm")
+        nc.vector.memset(warm[:], 0.0)
+        warm_out = keep.tile([P, 1], F32, name="warm_out")
+        nc.scalar.activation(warm_out[:], warm[:], ACT.Exp)
+
+        q_bf = keep.tile([P, Q, PACK], BF16, name="q_bf", align_bytes=64)
+        nc.vector.tensor_copy(q_bf[:], q_raw[:].rearrange("p j q -> p q j"))
+        q_codes = keep.tile([P, Q], U32, name="q_codes", align_bytes=64)
+        q_scales = keep.tile([P, Q], U8, name="q_scales", align_bytes=64)
+        nc.vector.quantize_mx(q_codes[:].bitcast(FP8X4), q_scales[:], q_bf[:].rearrange("p q j -> p (q j)"))
+
+        age_pool = keep.tile([P, T], F32, name="age_pool")
+        age_view = age_pool[:].rearrange("m (n j) -> m n j", j=T // P)
+        for c in range(4):
+            bank = turn.tile([P, 4, P], F32, name="bank")
+            for j in range(4):
+                col = 4 * c + j
+                nc.tensor.transpose(bank[:, j, :], age_cols[:, col : col + 1].to_broadcast([P, P]), ident[:])
+            nc.scalar.copy(age_view[:, :, 4 * c : 4 * c + 4], bank[:].rearrange("m j n -> m n j"))
+
+        size_bank = psum.tile([P, PACK, P], F32, name="size_bank")
+        for j in range(PACK):
+            nc.tensor.transpose(size_bank[:, j, :], size_cols[:, j : j + 1].to_broadcast([P, P]), ident[:])
+
+        k_scales = keep.tile([P, I], U8, name="k_scales", align_bytes=64)
+        nc.vector.tensor_copy(k_scales[:], kscale_pool[:].indirect(offsets[:]))
+        k_codes = keep.tile([P, I], U32, name="k_codes", align_bytes=64)
+        nc.vector.tensor_copy(k_codes[:], kword_pool[:].indirect(offsets[:]))
+        scores = psum.tile([P, I], F32, name="scores")
+        nc.tensor.matmul_mx(
+            scores[:], lhsT=q_codes[:].bitcast(FP8X4), lhsT_scale=q_scales[:],
+            rhs=k_codes[:].bitcast(FP8X4), rhs_scale=k_scales[:], start=True, stop=True,
+        )
+
+        slot_age = keep.tile([P, I], F32, name="slot_age")
+        nc.vector.tensor_copy(slot_age[:], age_pool[:].indirect(offsets[:]))
+
+        neg_max = keep.tile([P, 1], F32, name="neg_max")
+        nc.vector.tensor_reduce(neg_max[:], scores[:], AXIS.X, ALU.max, negate=True)
+        neg_z = keep.tile([P, I], F32, name="neg_z")
+        nc.vector.scalar_tensor_tensor(neg_z[:], slot_age[:], rate_col[:], scores[:], ALU.mult, ALU.subtract)
+        p = keep.tile([P, I], F32, name="p")
+        p_sum = keep.tile([P, 1], F32, name="p_sum")
+        nc.scalar.activation(p[:], neg_z[:], ACT.Exp, bias=neg_max[:], scale=-1.0, accum_out=p_sum[:])
+        denom = keep.tile([P, 1], F32, name="denom")
+        nc.vector.tensor_tensor(denom[:], p_sum[:], reserve_col[:], ALU.add)
+        inv = keep.tile([P, 1], F32, name="inv")
+        nc.vector.reciprocal(inv[:], denom[:])
+        w_bf = keep.tile([P, I], BF16, name="w_bf")
+        nc.vector.scalar_tensor_tensor(
+            w_bf[:].rearrange("q (n j) -> q n j", j=PACK), p[:].rearrange("q (n j) -> q n j", j=PACK), inv[:],
+            size_bank[:].rearrange("q j n -> q n j"), ALU.mult, ALU.mult,
+        )
+
+        def turn_slots(rows_bf, bank, grouped):
+            words = rows_bf[:].bitcast(F32)
+            for u in range(2):
+                nc.tensor.transpose(bank[:, u, :], words[:, u : I // 2 : 2], ident[:])
+            nc.scalar.copy(grouped.bitcast(F32).rearrange("p (c u) -> p c u", u=2), bank[:].rearrange("p u c -> p c u"))
+
+        w_grouped = keep.tile([P, Q * PACK], BF16, name="w_grouped", align_bytes=64)
+        turn_slots(w_bf, psum.tile([P, 2, P], F32, name="w_bank"), w_grouped[:])
+
+        v_grouped = [
+            keep.tile([P, 2 * P * PACK], BF16, name="v_grouped01", align_bytes=64),
+            keep.tile([P, P * PACK], BF16, name="v_grouped2", align_bytes=64),
+            keep.tile([P, P * PACK], BF16, name="v_grouped3", align_bytes=64),
+        ]
+        places = [v_grouped[0][:, 0 : P * PACK], v_grouped[0][:, P * PACK :], v_grouped[1][:], v_grouped[2][:]]
+        for b in range(E // P):
+            v_bf = keep.tile([P, I], BF16, name="v_bf%d" % b)
+            nc.vector.tensor_copy(v_bf[:], val_pool[b][:].indirect(offsets[:]))
+            turn_slots(v_bf, turn.tile([P, 2, P], F32, name="bank"), places[b])
+
+        head_codes = keep.tile([P, 3 * P], U32, name="head_codes", tag="val_pool2", align_bytes=64)
+        head_scales = keep.tile([P, 3 * P], U8, name="head_scales", align_bytes=64)
+        w_codes, w_scales = head_codes[:, 0:P], head_scales[:, 0:P]
+        nc.vector.quantize_mx(w_codes.bitcast(FP8X4), w_scales, w_grouped[:])
+        v_codes = [
+            head_codes[:, P:],
+            keep.tile([P, P], U32, name="v_codes2", tag="val_pool3", align_bytes=64)[:],
+            keep.tile([P, P], U32, name="v_codes3", align_bytes=64)[:],
+        ]
+        v_scales = [
+            head_scales[:, P:],
+            keep.tile([P, P], U8, name="v_scales2", align_bytes=64)[:],
+            keep.tile([P, P], U8, name="v_scales3", align_bytes=64)[:],
+        ]
+        edges = [0, 2 * P, 3 * P, E]
+        for s in range(3):
+            width = edges[s + 1] - edges[s]
+            nc.vector.quantize_mx(v_codes[s].bitcast(FP8X4), v_scales[s], v_grouped[s][:])
+            acc = psum.tile([P, width], F32, name="acc", tag="acc%d" % (s % 2))
+            nc.tensor.matmul_mx(
+                acc[:], lhsT=w_codes.bitcast(FP8X4), lhsT_scale=w_scales,
+                rhs=v_codes[s].bitcast(FP8X4), rhs_scale=v_scales[s], start=True, stop=True,
+            )
+            res = keep.tile([P, width], F32, name="res%d" % s)
+            if s < 2:
+                nc.scalar.copy(res[:], acc[:])
+            else:
+                nc.vector.tensor_copy(res[:], acc[:])
+            nc.sync.dma_start(out[:, edges[s] : edges[s + 1]], res[:])

@@ -38,16 +38,18 @@ def tile_attend_massfade_kernel(tc, query, keys_words, keys_scales, age, rate, r
 
         age_cols = keep.tile([P, T // P], F32, name="age_cols")
         nc.sync.dma_start(age_cols[:], age[0, :].rearrange("(p j) -> p j", p=P))
+        size_cols = keep.tile([P, PACK], F32, name="size_cols")
+        nc.sync.dma_start(size_cols[:], size[0, :].rearrange("(p j) -> p j", p=P))
         q_raw = keep.tile([P, PACK, Q], F32, name="q_raw")
         nc.sync.dma_start(q_raw[:], query.rearrange("(p j) q -> p j q", j=PACK))
+        kword_pool = keep.tile([P, T], U32, name="kword_pool")
+        words_hbm = keys_words[0].rearrange("p n t -> p (n t)").bitcast(I32)
+        nc.sync.dma_start(kword_pool[:, 0 : T // 4].bitcast(I32), words_hbm[:, 0 : T // 4])
         for g in range(4):
             nc.sync.dma_start(
                 kscale_pool[32 * g : 32 * g + 4, :].bitcast(I32), keys_scales[0, 4 * g : 4 * g + 4, :].bitcast(I32)
             )
-        kword_pool = keep.tile([P, T], U32, name="kword_pool")
-        nc.sync.dma_start(kword_pool[:].bitcast(I32), keys_words[0].rearrange("p n t -> p (n t)").bitcast(I32))
-        size_cols = keep.tile([P, PACK], F32, name="size_cols")
-        nc.sync.dma_start(size_cols[:], size[0, :].rearrange("(p j) -> p j", p=P))
+        nc.sync.dma_start(kword_pool[:, T // 4 : T].bitcast(I32), words_hbm[:, T // 4 : T])
         rate_col = keep.tile([P, 1], F32, name="rate_col")
         nc.sync.dma_start(rate_col[:], rate)
         reserve_col = keep.tile([P, 1], F32, name="reserve_col")
@@ -100,7 +102,9 @@ def tile_attend_massfade_kernel(tc, query, keys_words, keys_scales, age, rate, r
         nc.vector.tensor_reduce(neg_max[:], scores[:], AXIS.X, ALU.max, negate=True)
         neg_z = keep.tile([P, I], F32, name="neg_z")
         nc.vector.scalar_tensor_tensor(neg_z[:], slot_age[:], rate_col[:], scores[:], ALU.mult, ALU.subtract)
-        p = keep.tile([P, I], F32, name="p")
+        pool_bf = keep.tile([P, T], BF16, name="pool_bf")
+        nc.scalar.copy(pool_bf[:], val_pool[0][:])
+        p = keep.tile([P, I], F32, name="p", tag="val_pool0", align_bytes=64)
         p_sum = keep.tile([P, 1], F32, name="p_sum")
         nc.scalar.activation(p[:], neg_z[:], ACT.Exp, bias=neg_max[:], scale=-1.0, accum_out=p_sum[:])
         denom = keep.tile([P, 1], F32, name="denom")
@@ -119,46 +123,35 @@ def tile_attend_massfade_kernel(tc, query, keys_words, keys_scales, age, rate, r
                 nc.tensor.transpose(bank[:, u, :], words[:, u : I // 2 : 2], ident[:])
             nc.scalar.copy(grouped.bitcast(F32).rearrange("p (c u) -> p c u", u=2), bank[:].rearrange("p u c -> p c u"))
 
-        w_grouped = keep.tile([P, Q * PACK], BF16, name="w_grouped", align_bytes=64)
-        turn_slots(w_bf, psum.tile([P, 2, P], F32, name="w_bank"), w_grouped[:])
-
-        v_grouped = [
-            keep.tile([P, 2 * P * PACK], BF16, name="v_grouped01", align_bytes=64),
-            keep.tile([P, P * PACK], BF16, name="v_grouped2", align_bytes=64),
-            keep.tile([P, P * PACK], BF16, name="v_grouped3", align_bytes=64),
+        grouped = [
+            keep.tile([P, 2, P * PACK], BF16, name="grouped_w0", align_bytes=64),
+            keep.tile([P, 2, P * PACK], BF16, name="grouped_12", align_bytes=64),
+            keep.tile([P, 1, P * PACK], BF16, name="grouped_3", align_bytes=64),
         ]
-        places = [v_grouped[0][:, 0 : P * PACK], v_grouped[0][:, P * PACK :], v_grouped[1][:], v_grouped[2][:]]
+        places = [grouped[0][:, 1, :], grouped[1][:, 0, :], grouped[1][:, 1, :], grouped[2][:, 0, :]]
+        turn_slots(w_bf, psum.tile([P, 2, P], F32, name="w_bank"), grouped[0][:, 0, :])
         for b in range(E // P):
-            v_bf = keep.tile([P, I], BF16, name="v_bf%d" % b)
-            nc.vector.tensor_copy(v_bf[:], val_pool[b][:].indirect(offsets[:]))
+            v_bf = keep.tile([P, I], BF16, name="v_bf%d" % b, tag="neg_z" if b == 0 else "v_bf%d" % b)
+            if b == 0:
+                nc.scalar.activation(v_bf[:], pool_bf[:].indirect(offsets[:]), ACT.Copy)
+            else:
+                nc.vector.tensor_copy(v_bf[:], val_pool[b][:].indirect(offsets[:]))
             turn_slots(v_bf, turn.tile([P, 2, P], F32, name="bank"), places[b])
 
-        head_codes = keep.tile([P, 3 * P], U32, name="head_codes", tag="val_pool2", align_bytes=64)
-        head_scales = keep.tile([P, 3 * P], U8, name="head_scales", align_bytes=64)
-        w_codes, w_scales = head_codes[:, 0:P], head_scales[:, 0:P]
-        nc.vector.quantize_mx(w_codes.bitcast(FP8X4), w_scales, w_grouped[:])
-        v_codes = [
-            head_codes[:, P:],
-            keep.tile([P, P], U32, name="v_codes2", tag="val_pool3", align_bytes=64)[:],
-            keep.tile([P, P], U32, name="v_codes3", align_bytes=64)[:],
-        ]
-        v_scales = [
-            head_scales[:, P:],
-            keep.tile([P, P], U8, name="v_scales2", align_bytes=64)[:],
-            keep.tile([P, P], U8, name="v_scales3", align_bytes=64)[:],
-        ]
-        edges = [0, 2 * P, 3 * P, E]
-        for s in range(3):
-            width = edges[s + 1] - edges[s]
-            nc.vector.quantize_mx(v_codes[s].bitcast(FP8X4), v_scales[s], v_grouped[s][:])
-            acc = psum.tile([P, width], F32, name="acc", tag="acc%d" % (s % 2))
+        codes = keep.tile([P, 5 * P], U32, name="codes", tag="val_pool3", align_bytes=64)
+        scales = keep.tile([P, 5 * P], U8, name="scales", align_bytes=64)
+        for s, (lo, hi) in enumerate([(0, 1), (1, 3), (3, 4)]):
+            made = slice(2 * s * P, min(2 * s + 2, 5) * P)
+            nc.vector.quantize_mx(codes[:, made].bitcast(FP8X4), scales[:, made], grouped[s][:].rearrange("p b c -> p (b c)"))
+            moving = slice((lo + 1) * P, (hi + 1) * P)
+            acc = psum.tile([P, (hi - lo) * P], F32, name="acc", tag="acc%d" % (s % 2))
             nc.tensor.matmul_mx(
-                acc[:], lhsT=w_codes.bitcast(FP8X4), lhsT_scale=w_scales,
-                rhs=v_codes[s].bitcast(FP8X4), rhs_scale=v_scales[s], start=True, stop=True,
+                acc[:], lhsT=codes[:, 0:P].bitcast(FP8X4), lhsT_scale=scales[:, 0:P],
+                rhs=codes[:, moving].bitcast(FP8X4), rhs_scale=scales[:, moving], start=True, stop=True,
             )
-            res = keep.tile([P, width], F32, name="res%d" % s)
-            if s < 2:
+            res = keep.tile([P, (hi - lo) * P], F32, name="res%d" % s)
+            if s == 1:
                 nc.scalar.copy(res[:], acc[:])
             else:
                 nc.vector.tensor_copy(res[:], acc[:])
-            nc.sync.dma_start(out[:, edges[s] : edges[s + 1]], res[:])
+            nc.sync.dma_start(out[:, lo * P : hi * P], res[:])

from contextlib import ExitStack

import concourse.mybir as mybir
from concourse.masks import make_identity

D, T, I, Q, E = 512, 2048, 512, 128, 512
FLOPS = 2 * Q * I * D + 2 * Q * I * E
BYTES = 4 * (D * Q + T + 2 * Q + I + E * T + Q * E) + D * T + 16 * T + 2 * 128 * 32

F32 = mybir.dt.float32
BF16 = mybir.dt.bfloat16
I32 = mybir.dt.int32
U32 = mybir.dt.uint32
U16 = mybir.dt.uint16
U8 = mybir.dt.uint8
FP8X4 = mybir.dt.float8_e4m3fn_x4
ALU = mybir.AluOpType
ACT = mybir.ActivationFunctionType
AXIS = mybir.AxisListType

P = 128
PACK = 4
BANK = 512


def tile_attend_massfade_kernel(tc, query, keys_words, keys_scales, age, rate, reserve, size, vals, offs, out):
    nc = tc.nc
    with ExitStack() as ctx:
        keep = ctx.enter_context(tc.tile_pool(name="keep", bufs=1))
        turn = ctx.enter_context(tc.psum_pool(name="turn", bufs=3))
        psum = ctx.enter_context(tc.psum_pool(name="psum", bufs=1))

        offsets = keep.tile([P, I // 16], U16, name="offsets")
        nc.sync.dma_start(offsets[:], offs)

        kscale_pool = keep.tile([P, T], U8, name="kscale_pool")
        nc.gpsimd.memset(kscale_pool[:].bitcast(I32), 0)

        age_cols = keep.tile([P, T // P], F32, name="age_cols")
        nc.sync.dma_start(age_cols[:], age[0, :].rearrange("(p j) -> p j", p=P))
        size_cols = keep.tile([P, PACK], F32, name="size_cols")
        nc.sync.dma_start(size_cols[:], size[0, :].rearrange("(p j) -> p j", p=P))
        q_raw = keep.tile([P, PACK, Q], F32, name="q_raw")
        nc.sync.dma_start(q_raw[:], query.rearrange("(p j) q -> p j q", j=PACK))
        kword_pool = keep.tile([P, T], U32, name="kword_pool")
        words_hbm = keys_words[0].rearrange("p n t -> p (n t)").bitcast(I32)
        nc.sync.dma_start(kword_pool[:, 0 : T // 4].bitcast(I32), words_hbm[:, 0 : T // 4])
        for g in range(4):
            nc.sync.dma_start(
                kscale_pool[32 * g : 32 * g + 4, :].bitcast(I32), keys_scales[0, 4 * g : 4 * g + 4, :].bitcast(I32)
            )
        nc.sync.dma_start(kword_pool[:, T // 4 : T].bitcast(I32), words_hbm[:, T // 4 : T])
        rate_col = keep.tile([P, 1], F32, name="rate_col")
        nc.sync.dma_start(rate_col[:], rate)
        reserve_col = keep.tile([P, 1], F32, name="reserve_col")
        nc.sync.dma_start(reserve_col[:], reserve)
        val_pool = [keep.tile([P, T], F32, name="val_pool%d" % b, align_bytes=64) for b in range(E // P)]
        for b in range(E // P):
            nc.sync.dma_start(val_pool[b][:], vals[b * P : (b + 1) * P, :])

        ident = keep.tile([P, P], F32, name="ident")
        make_identity(nc, ident[:])

        warm = keep.tile([P, 1], F32, name="warm")
        nc.vector.memset(warm[:], 0.0)
        warm_out = keep.tile([P, 1], F32, name="warm_out")
        nc.scalar.activation(warm_out[:], warm[:], ACT.Exp)

        q_bf = keep.tile([P, Q, PACK], BF16, name="q_bf", align_bytes=64)
        nc.vector.tensor_copy(q_bf[:], q_raw[:].rearrange("p j q -> p q j"))
        q_codes = keep.tile([P, Q], U32, name="q_codes", align_bytes=64)
        q_scales = keep.tile([P, Q], U8, name="q_scales", align_bytes=64)
        nc.vector.quantize_mx(q_codes[:].bitcast(FP8X4), q_scales[:], q_bf[:].rearrange("p q j -> p (q j)"))

        age_pool = keep.tile([P, T], F32, name="age_pool")
        age_view = age_pool[:].rearrange("m (n j) -> m n j", j=T // P)
        for c in range(4):
            bank = turn.tile([P, 4, P], F32, name="bank")
            for j in range(4):
                col = 4 * c + j
                nc.tensor.transpose(bank[:, j, :], age_cols[:, col : col + 1].to_broadcast([P, P]), ident[:])
            nc.scalar.copy(age_view[:, :, 4 * c : 4 * c + 4], bank[:].rearrange("m j n -> m n j"))

        size_bank = psum.tile([P, PACK, P], F32, name="size_bank")
        for j in range(PACK):
            nc.tensor.transpose(size_bank[:, j, :], size_cols[:, j : j + 1].to_broadcast([P, P]), ident[:])

        k_scales = keep.tile([P, I], U8, name="k_scales", align_bytes=64)
        nc.vector.tensor_copy(k_scales[:], kscale_pool[:].indirect(offsets[:]))
        k_codes = keep.tile([P, I], U32, name="k_codes", align_bytes=64)
        nc.vector.tensor_copy(k_codes[:], kword_pool[:].indirect(offsets[:]))
        scores = psum.tile([P, I], F32, name="scores")
        nc.tensor.matmul_mx(
            scores[:], lhsT=q_codes[:].bitcast(FP8X4), lhsT_scale=q_scales[:],
            rhs=k_codes[:].bitcast(FP8X4), rhs_scale=k_scales[:], start=True, stop=True,
        )

        slot_age = keep.tile([P, I], F32, name="slot_age")
        nc.vector.tensor_copy(slot_age[:], age_pool[:].indirect(offsets[:]))

        neg_max = keep.tile([P, 1], F32, name="neg_max")
        nc.vector.tensor_reduce(neg_max[:], scores[:], AXIS.X, ALU.max, negate=True)
        neg_z = keep.tile([P, I], F32, name="neg_z")
        nc.vector.scalar_tensor_tensor(neg_z[:], slot_age[:], rate_col[:], scores[:], ALU.mult, ALU.subtract)
        pool_bf = keep.tile([P, T], BF16, name="pool_bf")
        nc.scalar.copy(pool_bf[:], val_pool[0][:])
        p = keep.tile([P, I], F32, name="p", tag="val_pool0", align_bytes=64)
        p_sum = keep.tile([P, 1], F32, name="p_sum")
        nc.scalar.activation(p[:], neg_z[:], ACT.Exp, bias=neg_max[:], scale=-1.0, accum_out=p_sum[:])
        denom = keep.tile([P, 1], F32, name="denom")
        nc.vector.tensor_tensor(denom[:], p_sum[:], reserve_col[:], ALU.add)
        inv = keep.tile([P, 1], F32, name="inv")
        nc.vector.reciprocal(inv[:], denom[:])
        w_bf = keep.tile([P, I], BF16, name="w_bf")
        nc.vector.scalar_tensor_tensor(
            w_bf[:].rearrange("q (n j) -> q n j", j=PACK), p[:].rearrange("q (n j) -> q n j", j=PACK), inv[:],
            size_bank[:].rearrange("q j n -> q n j"), ALU.mult, ALU.mult,
        )

        def turn_slots(rows_bf, bank, grouped):
            words = rows_bf[:].bitcast(F32)
            for u in range(2):
                nc.tensor.transpose(bank[:, u, :], words[:, u : I // 2 : 2], ident[:])
            nc.scalar.copy(grouped.bitcast(F32).rearrange("p (c u) -> p c u", u=2), bank[:].rearrange("p u c -> p c u"))

        grouped = [
            keep.tile([P, 2, P * PACK], BF16, name="grouped_w0", align_bytes=64),
            keep.tile([P, 2, P * PACK], BF16, name="grouped_12", align_bytes=64),
            keep.tile([P, 1, P * PACK], BF16, name="grouped_3", align_bytes=64),
        ]
        places = [grouped[0][:, 1, :], grouped[1][:, 0, :], grouped[1][:, 1, :], grouped[2][:, 0, :]]
        turn_slots(w_bf, psum.tile([P, 2, P], F32, name="w_bank"), grouped[0][:, 0, :])
        for b in range(E // P):
            v_bf = keep.tile([P, I], BF16, name="v_bf%d" % b, tag="neg_z" if b == 0 else "v_bf%d" % b)
            if b == 0:
                nc.scalar.activation(v_bf[:], pool_bf[:].indirect(offsets[:]), ACT.Copy)
            else:
                nc.vector.tensor_copy(v_bf[:], val_pool[b][:].indirect(offsets[:]))
            turn_slots(v_bf, turn.tile([P, 2, P], F32, name="bank"), places[b])

        codes = keep.tile([P, 5 * P], U32, name="codes", tag="val_pool3", align_bytes=64)
        scales = keep.tile([P, 5 * P], U8, name="scales", align_bytes=64)
        for s, (lo, hi) in enumerate([(0, 1), (1, 3), (3, 4)]):
            made = slice(2 * s * P, min(2 * s + 2, 5) * P)
            nc.vector.quantize_mx(codes[:, made].bitcast(FP8X4), scales[:, made], grouped[s][:].rearrange("p b c -> p (b c)"))
            moving = slice((lo + 1) * P, (hi + 1) * P)
            acc = psum.tile([P, (hi - lo) * P], F32, name="acc", tag="acc%d" % (s % 2))
            nc.tensor.matmul_mx(
                acc[:], lhsT=codes[:, 0:P].bitcast(FP8X4), lhsT_scale=scales[:, 0:P],
                rhs=codes[:, moving].bitcast(FP8X4), rhs_scale=scales[:, moving], start=True, stop=True,
            )
            res = keep.tile([P, (hi - lo) * P], F32, name="res%d" % s)
            if s == 1:
                nc.scalar.copy(res[:], acc[:])
            else:
                nc.vector.tensor_copy(res[:], acc[:])
            nc.sync.dma_start(out[:, lo * P : hi * P], res[:])
